import numpy as np
import ml_dtypes


def mxq(x, axis, fmt="e4m3"):
    dtype, down = {"e4m3": (ml_dtypes.float8_e4m3fn, 7), "e5m2": (ml_dtypes.float8_e5m2, 14)}[fmt]
    v = np.moveaxis(np.asarray(x, np.float32).astype(ml_dtypes.bfloat16).astype(np.float64), axis, -1)
    blocks = v.reshape(v.shape[:-1] + (-1, 32))
    amax = np.abs(blocks).max(-1, keepdims=True)
    byte = np.maximum(np.where(amax > 0, np.frexp(amax)[1] - 1 + 127, 0) - down, 1)
    scale = np.exp2(byte - 127.0)
    codes = (blocks / scale).astype(np.float32).astype(dtype).astype(np.float64)
    return np.moveaxis((codes * scale).reshape(v.shape), -1, axis)


WIDE = False


def mx_kscale(k):
    if not WIDE:
        return np.ones(k)
    levels = np.array([10, -10, 5, -5, 0])
    if k % 512:
        return np.exp2(np.random.permutation(np.resize(levels, k // 32))).repeat(32)
    a = np.empty((k // 512, 16))
    for p in range(k // 512):
        a[p, :8] = np.random.permutation(np.resize(levels, 8))
        for g in range(8):
            far = levels[np.abs(levels - a[p, g]) >= 10]
            a[p, g + 8] = far[np.random.randint(len(far))]
    return np.exp2(a.ravel()).repeat(32)


def f64(x):
    return np.asarray(x).astype(np.float64)


def striped(idx):
    return np.tile(idx.reshape(-1, 16).T, (8, 1)).astype(np.uint16)


def unstriped(offs):
    return offs[:16].T.reshape(-1).astype(np.int64)


def relu(v):
    return np.maximum(v, 0.0)


K, T, S, H, N = 512, 4096, 2048, 512, 256


def setup_inputs():
    n = np.random.standard_normal
    s = mx_kscale(K)[:, None]
    u = mx_kscale(H)
    return {
        "xT": (n((K, S)) * s).astype(np.float32),
        "w1": (n((K, H)) / np.sqrt(K) / s * u).astype(np.float32),
        "w2": (n((H, N)) / np.sqrt(H) / u[:, None]).astype(np.float32),
        "gate": np.tile(np.random.uniform(0.2, 1.0, S), (N, 1)).astype(np.float32),
        "offs": striped(np.sort(np.random.permutation(T)[:S])),
    }


def reference(xT, w1, w2, gate, offs):
    idx = unstriped(offs)
    xq = mxq(f64(xT), 0, "e4m3")
    h = relu(mxq(f64(w1), 0, "e4m3").T @ xq)
    y = mxq(f64(w2), 0, "e4m3").T @ mxq(h, 0, "e4m3")
    out = np.zeros((N, T))
    out[:, idx] = f64(gate) * y
    return out

@@ -1,0 +1,163 @@
+from contextlib import ExitStack
+
+import concourse.mybir as mybir
+
+K, T, S, H, N = 512, 4096, 2048, 512, 256
+FLOPS = 2 * S * (K * H + H * N)
+
+F32 = mybir.dt.float32
+BF16 = mybir.dt.bfloat16
+U32 = mybir.dt.uint32
+U16 = mybir.dt.uint16
+U8 = mybir.dt.uint8
+FP8X4 = mybir.dt.float8_e4m3fn_x4
+RELU = mybir.ActivationFunctionType.Relu
+MULT = mybir.AluOpType.mult
+
+P = 128
+C = 512
+NCH = S // C
+
+
+def tile_picked_place_mlp_relu_srt_l_kernel(tc, xT, w1, w2, gate, offs, out):
+    nc = tc.nc
+    x_hbm = xT.rearrange("(p j) s -> p j s", j=4)
+    w1_hbm = w1.rearrange("(p j) c -> p j c", j=4)
+    w2_hbm = w2.rearrange("(p j) c -> p j c", j=4)
+    gate_hbm = gate.rearrange("(b p) s -> p b s", p=P)
+    out_hbm = out.rearrange("(b p) t -> b p t", p=P)
+
+    with ExitStack() as ctx:
+        keep = ctx.enter_context(tc.tile_pool(name="keep", bufs=1))
+        acc1 = ctx.enter_context(tc.psum_pool(name="acc1", bufs=4))
+        acc2 = ctx.enter_context(tc.psum_pool(name="acc2", bufs=4))
+
+        offsets = keep.tile([P, S // 16], U16, name="offsets")
+        warm = keep.tile([P, 8], F32, name="warm")
+        nc.gpsimd.memset(warm[:], 0.0)
+        nc.scalar.activation(warm[:, 0:1], warm[:, 1:2], RELU)
+
+        def load(name, shape, src):
+            t = keep.tile(shape, F32, name=name, align_bytes=64)
+            nc.sync.dma_start(out=t[:], in_=src)
+            return t
+
+        w1_raw = [load(f"w1_raw{i}", [P, 4, 256], w1_hbm[:, :, 256 * i : 256 * i + 256]) for i in range(2)]
+        x_raw = [None] * NCH
+        g_raw = [None] * NCH
+
+        def load_x(c):
+            x_raw[c] = load(f"x_raw{c}", [P, 4, C], x_hbm[:, :, C * c : C * c + C])
+
+        def load_g(c):
+            g_raw[c] = load(f"g_raw{c}", [P, 2, C], gate_hbm[:, :, C * c : C * c + C])
+
+        load_x(0)
+        w2_raw = load("w2_raw", [P, 4, N], w2_hbm)
+        load_x(1)
+        nc.sync.dma_start(offsets[:], offs)
+        load_g(0)
+        load_x(2)
+        load_g(1)
+        load_x(3)
+        load_g(2)
+        load_g(3)
+
+        windows = [keep.tile([P, T], F32, name=f"window{b}", align_bytes=64) for b in range(2)]
+        nc.vector.memset(windows[0][:], 0.0)
+
+        w1_g = keep.tile([P, 4, P, 4], BF16, name="w1_g", align_bytes=64)
+        w1_q = keep.tile([P, H], U32, name="w1_q", align_bytes=64)
+        w1_s = keep.tile([P, H], U8, name="w1_s", align_bytes=64)
+        for i in range(2):
+            dst = w1_g[:, :, 64 * i : 64 * i + 64, :].rearrange("p t m j -> p m t j")
+            src = w1_raw[i][:].rearrange("p j (m t) -> p m t j", t=4)
+            if i == 0:
+                nc.vector.tensor_copy(out=dst, in_=src)
+            else:
+                nc.scalar.copy(out=dst, in_=src)
+        nc.vector.quantize_mx(out=w1_q[:].bitcast(FP8X4), scales=w1_s[:], in_=w1_g[:].rearrange("p t m j -> p (t m j)"))
+
+        x_g = [keep.tile([P, C, 4], BF16, name=f"x_g{c}", align_bytes=64) for c in range(NCH)]
+        x_q = [keep.tile([P, C], U32, name=f"x_q{c}", align_bytes=64) for c in range(NCH)]
+        x_s = [keep.tile([P, C], U8, name=f"x_s{c}", align_bytes=64) for c in range(NCH)]
+        h_g = [keep.tile([P, C, 4], BF16, name=f"h_g{c}", align_bytes=64) for c in range(NCH)]
+        h_q = [keep.tile([P, C], U32, name=f"h_q{c}", align_bytes=64) for c in range(NCH)]
+        h_s = [keep.tile([P, C], U8, name=f"h_s{c}", align_bytes=64) for c in range(NCH)]
+        y = [[keep.tile([P, C], F32, name=f"y{c}_{b}", align_bytes=64) for b in range(2)] for c in range(NCH)]
+
+        def interleave(copy, c, a, b):
+            copy(
+                out=x_g[c][:, a:b, :].rearrange("p (c i) j -> p c j i", i=4),
+                in_=x_raw[c][:, :, a:b].rearrange("p j (c i) -> p c j i", i=4),
+            )
+
+        def stage_x(c):
+            interleave(nc.scalar.copy, c, 0, XS[c])
+            interleave(nc.vector.tensor_copy, c, XS[c], C)
+            nc.vector.quantize_mx(out=x_q[c][:].bitcast(FP8X4), scales=x_s[c][:], in_=x_g[c][:].rearrange("p n j -> p (n j)"))
+
+        def layer1(c):
+            for s in range(4):
+                ps = acc1.tile([P, 4, P], F32, name="ps")
+                for t in range(4):
+                    nc.tensor.matmul_mx(
+                        out=ps[:, t, :],
+                        lhsT=w1_q[:, P * t : P * t + P].bitcast(FP8X4),
+                        lhsT_scale=w1_s[:, P * t : P * t + P],
+                        rhs=x_q[c][:, P * s : P * s + P].bitcast(FP8X4),
+                        rhs_scale=x_s[c][:, P * s : P * s + P],
+                        start=True,
+                        stop=True,
+                    )
+                nc.scalar.activation(h_g[c][:, P * s : P * s + P, :], ps[:].rearrange("p t n -> p n t"), RELU)
+
+        def stage_h(c):
+            nc.vector.quantize_mx(out=h_q[c][:].bitcast(FP8X4), scales=h_s[c][:], in_=h_g[c][:].rearrange("p n j -> p (n j)"))
+
+        def layer2(c):
+            for b in range(2):
+                py = acc2.tile([P, C], F32, name="py")
+                nc.tensor.matmul_mx(
+                    out=py[:],
+                    lhsT=w2_q[:, P * b : P * b + P].bitcast(FP8X4),
+                    lhsT_scale=w2_s[:, P * b : P * b + P],
+                    rhs=h_q[c][:].bitcast(FP8X4),
+                    rhs_scale=h_s[c][:],
+                    start=True,
+                    stop=True,
+                )
+                nc.scalar.copy(out=y[c][b][:], in_=py[:])
+
+        def scatter(c, b):
+            nc.vector.tensor_tensor(
+                windows[b][:].indirect(offsets[:, C // 16 * c : C // 16 * (c + 1)]), y[c][b][:], g_raw[c][:, b, :], MULT
+            )
+
+        XS = [256, 256, 256, 256]
+        stage_x(0)
+        nc.vector.memset(windows[1][:], 0.0)
+        layer1(0)
+        w2_g = keep.tile([P, N, 4], BF16, name="w2_g", align_bytes=64)
+        w2_q = keep.tile([P, N], U32, name="w2_q", align_bytes=64)
+        w2_s = keep.tile([P, N], U8, name="w2_s", align_bytes=64)
+        nc.vector.tensor_copy(
+            out=w2_g[:].rearrange("p (c i) j -> p c j i", i=4), in_=w2_raw[:].rearrange("p j (c i) -> p c j i", i=4)
+        )
+        nc.vector.quantize_mx(out=w2_q[:].bitcast(FP8X4), scales=w2_s[:], in_=w2_g[:].rearrange("p n j -> p (n j)"))
+        stage_x(1)
+        for c in range(NCH):
+            stage_h(c)
+            if c > 0:
+                scatter(c - 1, 0)
+            if c + 2 < NCH:
+                stage_x(c + 2)
+            if c + 1 < NCH:
+                layer1(c + 1)
+            if c > 0:
+                scatter(c - 1, 1)
+            layer2(c)
+        for b in range(2):
+            scatter(NCH - 1, b)
+            for i in range(2):
+                nc.sync.dma_start(out=out_hbm[b, :, 2048 * i : 2048 * i + 2048], in_=windows[b][:, 2048 * i : 2048 * i + 2048])

@@ -64,7 +64,6 @@ def tile_picked_place_mlp_relu_srt_l_kernel(tc, xT, w1, w2, gate, offs, out):
         load_g(3)
 
         windows = [keep.tile([P, T], F32, name=f"window{b}", align_bytes=64) for b in range(2)]
-        nc.vector.memset(windows[0][:], 0.0)
 
         w1_g = keep.tile([P, 4, P, 4], BF16, name="w1_g", align_bytes=64)
         w1_q = keep.tile([P, H], U32, name="w1_q", align_bytes=64)
@@ -87,17 +86,20 @@ def tile_picked_place_mlp_relu_srt_l_kernel(tc, xT, w1, w2, gate, offs, out):
         y = [[keep.tile([P, C], F32, name=f"y{c}_{b}", align_bytes=64) for b in range(2)] for c in range(NCH)]
 
         def interleave(copy, c, a, b):
-            copy(
-                out=x_g[c][:, a:b, :].rearrange("p (c i) j -> p c j i", i=4),
-                in_=x_raw[c][:, :, a:b].rearrange("p j (c i) -> p c j i", i=4),
-            )
+            if b > a:
+                copy(
+                    out=x_g[c][:, a:b, :].rearrange("p (c i) j -> p c j i", i=4),
+                    in_=x_raw[c][:, :, a:b].rearrange("p j (c i) -> p c j i", i=4),
+                )
+
+        XS = [256, 256, 384, 384]
 
         def stage_x(c):
             interleave(nc.scalar.copy, c, 0, XS[c])
             interleave(nc.vector.tensor_copy, c, XS[c], C)
             nc.vector.quantize_mx(out=x_q[c][:].bitcast(FP8X4), scales=x_s[c][:], in_=x_g[c][:].rearrange("p n j -> p (n j)"))
 
-        def layer1(c):
+        def layer1(c, v_banks):
             for s in range(4):
                 ps = acc1.tile([P, 4, P], F32, name="ps")
                 for t in range(4):
@@ -110,54 +112,57 @@ def tile_picked_place_mlp_relu_srt_l_kernel(tc, xT, w1, w2, gate, offs, out):
                         start=True,
                         stop=True,
                     )
-                nc.scalar.activation(h_g[c][:, P * s : P * s + P, :], ps[:].rearrange("p t n -> p n t"), RELU)
+                dst, src = h_g[c][:, P * s : P * s + P, :], ps[:].rearrange("p t n -> p n t")
+                if s in v_banks:
+                    nc.vector.tensor_scalar_max(dst, src, 0.0)
+                else:
+                    nc.scalar.activation(dst, src, RELU)
 
         def stage_h(c):
             nc.vector.quantize_mx(out=h_q[c][:].bitcast(FP8X4), scales=h_s[c][:], in_=h_g[c][:].rearrange("p n j -> p (n j)"))
 
-        def layer2(c):
-            for b in range(2):
-                py = acc2.tile([P, C], F32, name="py")
-                nc.tensor.matmul_mx(
-                    out=py[:],
-                    lhsT=w2_q[:, P * b : P * b + P].bitcast(FP8X4),
-                    lhsT_scale=w2_s[:, P * b : P * b + P],
-                    rhs=h_q[c][:].bitcast(FP8X4),
-                    rhs_scale=h_s[c][:],
-                    start=True,
-                    stop=True,
-                )
-                nc.scalar.copy(out=y[c][b][:], in_=py[:])
+        def layer2(c, b, copy):
+            py = acc2.tile([P, C], F32, name="py")
+            nc.tensor.matmul_mx(
+                out=py[:],
+                lhsT=w2_q[:, P * b : P * b + P].bitcast(FP8X4),
+                lhsT_scale=w2_s[:, P * b : P * b + P],
+                rhs=h_q[c][:].bitcast(FP8X4),
+                rhs_scale=h_s[c][:],
+                start=True,
+                stop=True,
+            )
+            copy(out=y[c][b][:], in_=py[:])
 
         def scatter(c, b):
             nc.vector.tensor_tensor(
                 windows[b][:].indirect(offsets[:, C // 16 * c : C // 16 * (c + 1)]), y[c][b][:], g_raw[c][:, b, :], MULT
             )
 
-        XS = [256, 256, 256, 256]
         stage_x(0)
-        nc.vector.memset(windows[1][:], 0.0)
-        layer1(0)
+        for i in range(8):
+            nc.vector.memset(windows[i // 4][:, 1024 * (i % 4) : 1024 * (i % 4) + 1024], 0.0)
         w2_g = keep.tile([P, N, 4], BF16, name="w2_g", align_bytes=64)
         w2_q = keep.tile([P, N], U32, name="w2_q", align_bytes=64)
         w2_s = keep.tile([P, N], U8, name="w2_s", align_bytes=64)
         nc.vector.tensor_copy(
             out=w2_g[:].rearrange("p (c i) j -> p c j i", i=4), in_=w2_raw[:].rearrange("p j (c i) -> p c j i", i=4)
         )
+        layer1(0, (1, 3))
         nc.vector.quantize_mx(out=w2_q[:].bitcast(FP8X4), scales=w2_s[:], in_=w2_g[:].rearrange("p n j -> p (n j)"))
-        stage_x(1)
+        STORES = {1: (0, 1024), 2: (1024, 1536), 3: (1536, 4096)}
         for c in range(NCH):
             stage_h(c)
-            if c > 0:
-                scatter(c - 1, 0)
+            if c == 0:
+                stage_x(1)
             if c + 2 < NCH:
                 stage_x(c + 2)
+            layer2(c, 0, nc.scalar.copy)
+            layer2(c, 1, nc.vector.tensor_copy if c in (0, 3) else nc.scalar.copy)
             if c + 1 < NCH:
-                layer1(c + 1)
-            if c > 0:
-                scatter(c - 1, 1)
-            layer2(c)
-        for b in range(2):
-            scatter(NCH - 1, b)
-            for i in range(2):
-                nc.sync.dma_start(out=out_hbm[b, :, 2048 * i : 2048 * i + 2048], in_=windows[b][:, 2048 * i : 2048 * i + 2048])
+                layer1(c + 1, ())
+            for b in range(2):
+                scatter(c, b)
+                if c in STORES:
+                    lo, hi = STORES[c]
+                    nc.sync.dma_start(out=out_hbm[b, :, lo:hi], in_=windows[b][:, lo:hi])

@@ -29,8 +29,8 @@ def tile_picked_place_mlp_relu_srt_l_kernel(tc, xT, w1, w2, gate, offs, out):
 
     with ExitStack() as ctx:
         keep = ctx.enter_context(tc.tile_pool(name="keep", bufs=1))
-        acc1 = ctx.enter_context(tc.psum_pool(name="acc1", bufs=4))
-        acc2 = ctx.enter_context(tc.psum_pool(name="acc2", bufs=4))
+        acc1 = ctx.enter_context(tc.psum_pool(name="acc1", bufs=5))
+        acc2 = ctx.enter_context(tc.psum_pool(name="acc2", bufs=3))
 
         offsets = keep.tile([P, S // 16], U16, name="offsets")
         warm = keep.tile([P, 8], F32, name="warm")
@@ -42,41 +42,46 @@ def tile_picked_place_mlp_relu_srt_l_kernel(tc, xT, w1, w2, gate, offs, out):
             nc.sync.dma_start(out=t[:], in_=src)
             return t
 
-        w1_raw = [load(f"w1_raw{i}", [P, 4, 256], w1_hbm[:, :, 256 * i : 256 * i + 256]) for i in range(2)]
-        x_raw = [None] * NCH
-        g_raw = [None] * NCH
+        x_raw = {}
+        g_raw = {}
+        w1_raw = {}
 
         def load_x(c):
             x_raw[c] = load(f"x_raw{c}", [P, 4, C], x_hbm[:, :, C * c : C * c + C])
 
+        def load_xh(c, h):
+            if h == 0 or (c not in x_raw):
+                x_raw[c] = x_raw.get(c) or keep.tile([P, 4, C], F32, name=f"x_raw{c}", align_bytes=64)
+            a = 256 * h
+            nc.sync.dma_start(out=x_raw[c][:, :, a : a + 256], in_=x_hbm[:, :, C * c + a : C * c + a + 256])
+
         def load_g(c):
             g_raw[c] = load(f"g_raw{c}", [P, 2, C], gate_hbm[:, :, C * c : C * c + C])
 
+        def load_w1(i):
+            w1_raw[i] = load(f"w1_raw{i}", [P, 4, 256], w1_hbm[:, :, 256 * i : 256 * i + 256])
+
         load_x(0)
-        w2_raw = load("w2_raw", [P, 4, N], w2_hbm)
-        load_x(1)
         nc.sync.dma_start(offsets[:], offs)
-        load_g(0)
+        load_w1(0)
+        load_w1(1)
+        load_xh(1, 1)
+        load_xh(1, 0)
+        w2_raw = load("w2_raw", [P, 4, N], w2_hbm)
         load_x(2)
-        load_g(1)
+        load_g(0)
         load_x(3)
+        load_g(1)
         load_g(2)
         load_g(3)
 
         windows = [keep.tile([P, T], F32, name=f"window{b}", align_bytes=64) for b in range(2)]
-
         w1_g = keep.tile([P, 4, P, 4], BF16, name="w1_g", align_bytes=64)
         w1_q = keep.tile([P, H], U32, name="w1_q", align_bytes=64)
         w1_s = keep.tile([P, H], U8, name="w1_s", align_bytes=64)
-        for i in range(2):
-            dst = w1_g[:, :, 64 * i : 64 * i + 64, :].rearrange("p t m j -> p m t j")
-            src = w1_raw[i][:].rearrange("p j (m t) -> p m t j", t=4)
-            if i == 0:
-                nc.vector.tensor_copy(out=dst, in_=src)
-            else:
-                nc.scalar.copy(out=dst, in_=src)
-        nc.vector.quantize_mx(out=w1_q[:].bitcast(FP8X4), scales=w1_s[:], in_=w1_g[:].rearrange("p t m j -> p (t m j)"))
-
+        w2_g = keep.tile([P, N, 4], BF16, name="w2_g", align_bytes=64)
+        w2_q = keep.tile([P, N], U32, name="w2_q", align_bytes=64)
+        w2_s = keep.tile([P, N], U8, name="w2_s", align_bytes=64)
         x_g = [keep.tile([P, C, 4], BF16, name=f"x_g{c}", align_bytes=64) for c in range(NCH)]
         x_q = [keep.tile([P, C], U32, name=f"x_q{c}", align_bytes=64) for c in range(NCH)]
         x_s = [keep.tile([P, C], U8, name=f"x_s{c}", align_bytes=64) for c in range(NCH)]
@@ -84,44 +89,61 @@ def tile_picked_place_mlp_relu_srt_l_kernel(tc, xT, w1, w2, gate, offs, out):
         h_q = [keep.tile([P, C], U32, name=f"h_q{c}", align_bytes=64) for c in range(NCH)]
         h_s = [keep.tile([P, C], U8, name=f"h_s{c}", align_bytes=64) for c in range(NCH)]
         y = [[keep.tile([P, C], F32, name=f"y{c}_{b}", align_bytes=64) for b in range(2)] for c in range(NCH)]
+        V, A = nc.vector.tensor_copy, nc.scalar.copy
 
-        def interleave(copy, c, a, b):
-            if b > a:
-                copy(
-                    out=x_g[c][:, a:b, :].rearrange("p (c i) j -> p c j i", i=4),
-                    in_=x_raw[c][:, :, a:b].rearrange("p j (c i) -> p c j i", i=4),
+        def ix(c, a, b, copy):
+            copy(
+                out=x_g[c][:, a:b, :].rearrange("p (c i) j -> p c j i", i=4),
+                in_=x_raw[c][:, :, a:b].rearrange("p j (c i) -> p c j i", i=4),
+            )
+
+        def qx(c, a=0, b=C):
+            nc.vector.quantize_mx(
+                out=x_q[c][:, a:b].bitcast(FP8X4), scales=x_s[c][:, a:b], in_=x_g[c][:, a:b, :].rearrange("p n j -> p (n j)")
+            )
+
+        def qh(c, a=0, b=C):
+            nc.vector.quantize_mx(
+                out=h_q[c][:, a:b].bitcast(FP8X4), scales=h_s[c][:, a:b], in_=h_g[c][:, a:b, :].rearrange("p n j -> p (n j)")
+            )
+
+        def iw1(i, copy):
+            copy(
+                out=w1_g[:, :, 64 * i : 64 * i + 64, :].rearrange("p t m j -> p m t j"),
+                in_=w1_raw[i][:].rearrange("p j (m t) -> p m t j", t=4),
+            )
+
+        def qw1():
+            nc.vector.quantize_mx(out=w1_q[:].bitcast(FP8X4), scales=w1_s[:], in_=w1_g[:].rearrange("p t m j -> p (t m j)"))
+
+        def w2p(copy=V):
+            copy(
+                out=w2_g[:].rearrange("p (c i) j -> p c j i", i=4), in_=w2_raw[:].rearrange("p j (c i) -> p c j i", i=4)
+            )
+            nc.vector.quantize_mx(out=w2_q[:].bitcast(FP8X4), scales=w2_s[:], in_=w2_g[:].rearrange("p n j -> p (n j)"))
+
+        def z(i):
+            nc.vector.memset(windows[i // 4][:, 1024 * (i % 4) : 1024 * (i % 4) + 1024], 0.0)
+
+        def l1(c, s, e):
+            ps = acc1.tile([P, 4, P], F32, name="ps")
+            for t in range(4):
+                nc.tensor.matmul_mx(
+                    out=ps[:, t, :],
+                    lhsT=w1_q[:, P * t : P * t + P].bitcast(FP8X4),
+                    lhsT_scale=w1_s[:, P * t : P * t + P],
+                    rhs=x_q[c][:, P * s : P * s + P].bitcast(FP8X4),
+                    rhs_scale=x_s[c][:, P * s : P * s + P],
+                    start=True,
+                    stop=True,
                 )
+            dst, src = h_g[c][:, P * s : P * s + P, :], ps[:].rearrange("p t n -> p n t")
+            if e == 1:
+                nc.vector.tensor_scalar_max(dst, src, 0.0)
+            else:
+                nc.scalar.activation(dst, src, RELU)
 
-        XS = [256, 256, 384, 384]
-
-        def stage_x(c):
-            interleave(nc.scalar.copy, c, 0, XS[c])
-            interleave(nc.vector.tensor_copy, c, XS[c], C)
-            nc.vector.quantize_mx(out=x_q[c][:].bitcast(FP8X4), scales=x_s[c][:], in_=x_g[c][:].rearrange("p n j -> p (n j)"))
-
-        def layer1(c, v_banks):
-            for s in range(4):
-                ps = acc1.tile([P, 4, P], F32, name="ps")
-                for t in range(4):
-                    nc.tensor.matmul_mx(
-                        out=ps[:, t, :],
-                        lhsT=w1_q[:, P * t : P * t + P].bitcast(FP8X4),
-                        lhsT_scale=w1_s[:, P * t : P * t + P],
-                        rhs=x_q[c][:, P * s : P * s + P].bitcast(FP8X4),
-                        rhs_scale=x_s[c][:, P * s : P * s + P],
-                        start=True,
-                        stop=True,
-                    )
-                dst, src = h_g[c][:, P * s : P * s + P, :], ps[:].rearrange("p t n -> p n t")
-                if s in v_banks:
-                    nc.vector.tensor_scalar_max(dst, src, 0.0)
-                else:
-                    nc.scalar.activation(dst, src, RELU)
-
-        def stage_h(c):
-            nc.vector.quantize_mx(out=h_q[c][:].bitcast(FP8X4), scales=h_s[c][:], in_=h_g[c][:].rearrange("p n j -> p (n j)"))
-
-        def layer2(c, b, copy):
+        def l2(c, b, copy):
             py = acc2.tile([P, C], F32, name="py")
             nc.tensor.matmul_mx(
                 out=py[:],
@@ -134,35 +156,73 @@ def tile_picked_place_mlp_relu_srt_l_kernel(tc, xT, w1, w2, gate, offs, out):
             )
             copy(out=y[c][b][:], in_=py[:])
 
-        def scatter(c, b):
+        def sc(c, b, *stores):
             nc.vector.tensor_tensor(
                 windows[b][:].indirect(offsets[:, C // 16 * c : C // 16 * (c + 1)]), y[c][b][:], g_raw[c][:, b, :], MULT
             )
+            for lo, hi in stores:
+                nc.sync.dma_start(out=out_hbm[b, :, lo:hi], in_=windows[b][:, lo:hi])
 
-        stage_x(0)
-        for i in range(8):
-            nc.vector.memset(windows[i // 4][:, 1024 * (i % 4) : 1024 * (i % 4) + 1024], 0.0)
-        w2_g = keep.tile([P, N, 4], BF16, name="w2_g", align_bytes=64)
-        w2_q = keep.tile([P, N], U32, name="w2_q", align_bytes=64)
-        w2_s = keep.tile([P, N], U8, name="w2_s", align_bytes=64)
-        nc.vector.tensor_copy(
-            out=w2_g[:].rearrange("p (c i) j -> p c j i", i=4), in_=w2_raw[:].rearrange("p j (c i) -> p c j i", i=4)
-        )
-        layer1(0, (1, 3))
-        nc.vector.quantize_mx(out=w2_q[:].bitcast(FP8X4), scales=w2_s[:], in_=w2_g[:].rearrange("p n j -> p (n j)"))
-        STORES = {1: (0, 1024), 2: (1024, 1536), 3: (1536, 4096)}
-        for c in range(NCH):
-            stage_h(c)
-            if c == 0:
-                stage_x(1)
-            if c + 2 < NCH:
-                stage_x(c + 2)
-            layer2(c, 0, nc.scalar.copy)
-            layer2(c, 1, nc.vector.tensor_copy if c in (0, 3) else nc.scalar.copy)
-            if c + 1 < NCH:
-                layer1(c + 1, ())
-            for b in range(2):
-                scatter(c, b)
-                if c in STORES:
-                    lo, hi = STORES[c]
-                    nc.sync.dma_start(out=out_hbm[b, :, lo:hi], in_=windows[b][:, lo:hi])
+        ix(0, 0, 256, A)
+        ix(0, 256, 384, A)
+        ix(0, 384, 512, V)
+        qx(0, 0, 256)
+        qx(0, 256, 512)
+        iw1(0, A)
+        iw1(1, A)
+        qw1()
+        z(0)
+        z(1)
+        z(2)
+        z(3)
+        z(4)
+        z(5)
+        z(6)
+        z(7)
+        l1(0, 0, 0)
+        l1(0, 1, 0)
+        l1(0, 2, 0)
+        l1(0, 3, 0)
+        ix(1, 0, 256, V)
+        ix(1, 256, 512, A)
+        qx(1, 0, 256)
+        qx(1, 256, 512)
+        w2p()
+        qh(0, 0, 256)
+        qh(0, 256, 512)
+        l2(0, 0, A)
+        l2(0, 1, A)
+        l1(1, 0, 0)
+        l1(1, 1, 1)
+        l1(1, 2, 0)
+        l1(1, 3, 0)
+        ix(2, 0, 256, A)
+        ix(2, 256, 512, V)
+        sc(0, 1)
+        sc(0, 0)
+        qx(2)
+        qh(1)
+        l2(1, 0, A)
+        sc(1, 0, (0, 1024))
+        l2(1, 1, A)
+        l1(2, 0, 0)
+        l1(2, 1, 0)
+        l1(2, 2, 0)
+        l1(2, 3, 0)
+        ix(3, 0, 512, A)
+        qx(3)
+        sc(1, 1, (0, 1024))
+        qh(2)
+        l2(2, 0, A)
+        l2(2, 1, A)
+        l1(3, 0, 1)
+        l1(3, 1, 0)
+        l1(3, 2, 0)
+        l1(3, 3, 0)
+        qh(3)
+        sc(2, 1, (1024, 1536))
+        sc(2, 0)
+        l2(3, 0, A)
+        sc(3, 0, (1024, 4096))
+        l2(3, 1, V)
+        sc(3, 1, (1536, 4096))

@@ -29,8 +29,8 @@ def tile_picked_place_mlp_relu_srt_l_kernel(tc, xT, w1, w2, gate, offs, out):
 
     with ExitStack() as ctx:
         keep = ctx.enter_context(tc.tile_pool(name="keep", bufs=1))
-        acc1 = ctx.enter_context(tc.psum_pool(name="acc1", bufs=5))
-        acc2 = ctx.enter_context(tc.psum_pool(name="acc2", bufs=3))
+        acc1 = ctx.enter_context(tc.psum_pool(name="acc1", bufs=6))
+        acc2 = ctx.enter_context(tc.psum_pool(name="acc2", bufs=2))
 
         offsets = keep.tile([P, S // 16], U16, name="offsets")
         warm = keep.tile([P, 8], F32, name="warm")
@@ -61,19 +61,19 @@ def tile_picked_place_mlp_relu_srt_l_kernel(tc, xT, w1, w2, gate, offs, out):
         def load_w1(i):
             w1_raw[i] = load(f"w1_raw{i}", [P, 4, 256], w1_hbm[:, :, 256 * i : 256 * i + 256])
 
-        load_x(0)
-        nc.sync.dma_start(offsets[:], offs)
+        load_xh(0, 1)
         load_w1(0)
         load_w1(1)
-        load_xh(1, 1)
-        load_xh(1, 0)
+        load_xh(0, 0)
+        load_x(1)
         w2_raw = load("w2_raw", [P, 4, N], w2_hbm)
-        load_x(2)
-        load_g(0)
-        load_x(3)
-        load_g(1)
-        load_g(2)
+        nc.sync.dma_start(offsets[:], offs)
         load_g(3)
+        load_g(0)
+        load_x(2)
+        load_g(1)
+        load_x(3)
+        load_g(2)
 
         windows = [keep.tile([P, T], F32, name=f"window{b}", align_bytes=64) for b in range(2)]
         w1_g = keep.tile([P, 4, P, 4], BF16, name="w1_g", align_bytes=64)
@@ -93,8 +93,8 @@ def tile_picked_place_mlp_relu_srt_l_kernel(tc, xT, w1, w2, gate, offs, out):
 
         def ix(c, a, b, copy):
             copy(
-                out=x_g[c][:, a:b, :].rearrange("p (c i) j -> p c j i", i=4),
-                in_=x_raw[c][:, :, a:b].rearrange("p j (c i) -> p c j i", i=4),
+                out=x_g[c][:, a:b, :],
+                in_=x_raw[c][:, :, a:b].rearrange("p j n -> p n j"),
             )
 
         def qx(c, a=0, b=C):
@@ -109,8 +109,8 @@ def tile_picked_place_mlp_relu_srt_l_kernel(tc, xT, w1, w2, gate, offs, out):
 
         def iw1(i, copy):
             copy(
-                out=w1_g[:, :, 64 * i : 64 * i + 64, :].rearrange("p t m j -> p m t j"),
-                in_=w1_raw[i][:].rearrange("p j (m t) -> p m t j", t=4),
+                out=w1_g[:, :, 64 * i : 64 * i + 64, :],
+                in_=w1_raw[i][:].rearrange("p j (m t) -> p t m j", t=4),
             )
 
         def qw1():
@@ -118,7 +118,7 @@ def tile_picked_place_mlp_relu_srt_l_kernel(tc, xT, w1, w2, gate, offs, out):
 
         def w2p(copy=V):
             copy(
-                out=w2_g[:].rearrange("p (c i) j -> p c j i", i=4), in_=w2_raw[:].rearrange("p j (c i) -> p c j i", i=4)
+                out=w2_g[:], in_=w2_raw[:].rearrange("p j n -> p n j")
             )
             nc.vector.quantize_mx(out=w2_q[:].bitcast(FP8X4), scales=w2_s[:], in_=w2_g[:].rearrange("p n j -> p (n j)"))
 
@@ -163,14 +163,13 @@ def tile_picked_place_mlp_relu_srt_l_kernel(tc, xT, w1, w2, gate, offs, out):
             for lo, hi in stores:
                 nc.sync.dma_start(out=out_hbm[b, :, lo:hi], in_=windows[b][:, lo:hi])
 
+        iw1(0, A)
+        iw1(1, V)
+        qw1()
         ix(0, 0, 256, A)
-        ix(0, 256, 384, A)
-        ix(0, 384, 512, V)
+        ix(0, 256, 512, A)
         qx(0, 0, 256)
         qx(0, 256, 512)
-        iw1(0, A)
-        iw1(1, A)
-        qw1()
         z(0)
         z(1)
         z(2)
@@ -183,46 +182,50 @@ def tile_picked_place_mlp_relu_srt_l_kernel(tc, xT, w1, w2, gate, offs, out):
         l1(0, 1, 0)
         l1(0, 2, 0)
         l1(0, 3, 0)
-        ix(1, 0, 256, V)
-        ix(1, 256, 512, A)
+        ix(1, 0, 128, A)
+        ix(1, 128, 256, V)
+        ix(1, 256, 512, V)
         qx(1, 0, 256)
         qx(1, 256, 512)
         w2p()
-        qh(0, 0, 256)
-        qh(0, 256, 512)
+        qh(0)
         l2(0, 0, A)
         l2(0, 1, A)
-        l1(1, 0, 0)
-        l1(1, 1, 1)
+        l1(1, 0, 1)
+        l1(1, 1, 0)
         l1(1, 2, 0)
         l1(1, 3, 0)
-        ix(2, 0, 256, A)
-        ix(2, 256, 512, V)
         sc(0, 1)
-        sc(0, 0)
-        qx(2)
-        qh(1)
+        ix(2, 0, 256, A)
+        ix(2, 256, 512, A)
+        qx(2, 0, 256)
+        qx(2, 256, 512)
+        qh(1, 0, 256)
+        qh(1, 256, 512)
         l2(1, 0, A)
-        sc(1, 0, (0, 1024))
         l2(1, 1, A)
         l1(2, 0, 0)
         l1(2, 1, 0)
+        sc(0, 0)
         l1(2, 2, 0)
         l1(2, 3, 0)
-        ix(3, 0, 512, A)
+        ix(3, 0, 256, V)
+        sc(1, 0, (0, 1024))
+        ix(3, 256, 512, A)
         qx(3)
         sc(1, 1, (0, 1024))
         qh(2)
         l2(2, 0, A)
-        l2(2, 1, A)
-        l1(3, 0, 1)
-        l1(3, 1, 0)
-        l1(3, 2, 0)
-        l1(3, 3, 0)
-        qh(3)
-        sc(2, 1, (1024, 1536))
         sc(2, 0)
+        l2(2, 1, A)
+        l1(3, 0, 0)
+        l1(3, 1, 0)
+        sc(2, 1, (1024, 1536))
+        l1(3, 2, 0)
+        l1(3, 3, 1)
+        qh(3, 0, 256)
+        qh(3, 256, 512)
         l2(3, 0, A)
+        l2(3, 1, A)
         sc(3, 0, (1024, 4096))
-        l2(3, 1, V)
         sc(3, 1, (1536, 4096))

@@ -17,6 +17,7 @@ MULT = mybir.AluOpType.mult
 P = 128
 C = 512
 NCH = S // C
+ZCUTS = [0, 1023, 2048, 3071, 4096]
 
 
 def tile_picked_place_mlp_relu_srt_l_kernel(tc, xT, w1, w2, gate, offs, out):
@@ -61,19 +62,20 @@ def tile_picked_place_mlp_relu_srt_l_kernel(tc, xT, w1, w2, gate, offs, out):
         def load_w1(i):
             w1_raw[i] = load(f"w1_raw{i}", [P, 4, 256], w1_hbm[:, :, 256 * i : 256 * i + 256])
 
-        load_xh(0, 1)
-        load_w1(0)
         load_w1(1)
+        load_w1(0)
         load_xh(0, 0)
-        load_x(1)
+        load_xh(0, 1)
+        load_xh(1, 0)
+        load_xh(1, 1)
         w2_raw = load("w2_raw", [P, 4, N], w2_hbm)
-        nc.sync.dma_start(offsets[:], offs)
-        load_g(3)
-        load_g(0)
         load_x(2)
-        load_g(1)
         load_x(3)
+        nc.sync.dma_start(offsets[:], offs)
+        load_g(0)
+        load_g(1)
         load_g(2)
+        load_g(3)
 
         windows = [keep.tile([P, T], F32, name=f"window{b}", align_bytes=64) for b in range(2)]
         w1_g = keep.tile([P, 4, P, 4], BF16, name="w1_g", align_bytes=64)
@@ -123,7 +125,9 @@ def tile_picked_place_mlp_relu_srt_l_kernel(tc, xT, w1, w2, gate, offs, out):
             nc.vector.quantize_mx(out=w2_q[:].bitcast(FP8X4), scales=w2_s[:], in_=w2_g[:].rearrange("p n j -> p (n j)"))
 
         def z(i):
-            nc.vector.memset(windows[i // 4][:, 1024 * (i % 4) : 1024 * (i % 4) + 1024], 0.0)
+            engine = nc.gpsimd if i >= 4 else nc.vector
+            a, b = ZCUTS[i % 4], ZCUTS[i % 4 + 1]
+            engine.memset(windows[i // 4][:, a:b], 0.0)
 
         def l1(c, s, e):
             ps = acc1.tile([P, 4, P], F32, name="ps")
@@ -163,12 +167,17 @@ def tile_picked_place_mlp_relu_srt_l_kernel(tc, xT, w1, w2, gate, offs, out):
             for lo, hi in stores:
                 nc.sync.dma_start(out=out_hbm[b, :, lo:hi], in_=windows[b][:, lo:hi])
 
-        iw1(0, A)
-        iw1(1, V)
-        qw1()
-        ix(0, 0, 256, A)
-        ix(0, 256, 512, A)
+        ix(1, 0, 128, V)
+        ix(1, 128, 256, A)
+        qx(1, 0, 256)
+        ix(0, 0, 128, V)
+        ix(0, 128, 256, A)
         qx(0, 0, 256)
+        ix(1, 256, 384, V)
+        ix(1, 384, 512, A)
+        qx(1, 256, 512)
+        ix(0, 256, 384, V)
+        ix(0, 384, 512, A)
         qx(0, 256, 512)
         z(0)
         z(1)
@@ -178,54 +187,52 @@ def tile_picked_place_mlp_relu_srt_l_kernel(tc, xT, w1, w2, gate, offs, out):
         z(5)
         z(6)
         z(7)
+        iw1(0, V)
+        iw1(1, A)
+        qw1()
+        ix(3, 0, 256, V)
+        qx(3, 0, 256)
+        l1(0, 2, 1)
+        l1(0, 3, 0)
+        w2p()
         l1(0, 0, 0)
         l1(0, 1, 0)
-        l1(0, 2, 0)
-        l1(0, 3, 0)
-        ix(1, 0, 128, A)
-        ix(1, 128, 256, V)
-        ix(1, 256, 512, V)
-        qx(1, 0, 256)
-        qx(1, 256, 512)
-        w2p()
+        l1(1, 0, 0)
+        l1(1, 1, 0)
         qh(0)
         l2(0, 0, A)
-        l2(0, 1, A)
-        l1(1, 0, 1)
-        l1(1, 1, 0)
         l1(1, 2, 0)
         l1(1, 3, 0)
-        sc(0, 1)
-        ix(2, 0, 256, A)
-        ix(2, 256, 512, A)
+        ix(2, 0, 256, V)
         qx(2, 0, 256)
+        qh(1)
+        l2(0, 1, A)
+        ix(2, 256, 384, V)
+        ix(2, 384, 512, A)
         qx(2, 256, 512)
-        qh(1, 0, 256)
-        qh(1, 256, 512)
         l2(1, 0, A)
-        l2(1, 1, A)
         l1(2, 0, 0)
         l1(2, 1, 0)
+        ix(3, 256, 512, V)
+        qx(3, 256, 512)
         sc(0, 0)
+        sc(1, 0, (0, 1024))
         l1(2, 2, 0)
         l1(2, 3, 0)
-        ix(3, 0, 256, V)
-        sc(1, 0, (0, 1024))
-        ix(3, 256, 512, A)
-        qx(3)
-        sc(1, 1, (0, 1024))
+        l2(1, 1, A)
+        sc(0, 1)
         qh(2)
-        l2(2, 0, A)
-        sc(2, 0)
-        l2(2, 1, A)
         l1(3, 0, 0)
         l1(3, 1, 0)
-        sc(2, 1, (1024, 1536))
         l1(3, 2, 0)
-        l1(3, 3, 1)
-        qh(3, 0, 256)
-        qh(3, 256, 512)
+        l1(3, 3, 0)
+        l2(2, 0, A)
+        sc(1, 1, (0, 1024))
+        qh(3)
+        sc(2, 0)
+        l2(2, 1, V)
         l2(3, 0, A)
-        l2(3, 1, A)
         sc(3, 0, (1024, 4096))
-        sc(3, 1, (1536, 4096))
+        l2(3, 1, A)
+        sc(2, 1)
+        sc(3, 1, (1024, 4096))

from contextlib import ExitStack

import concourse.mybir as mybir

K, T, S, H, N = 512, 4096, 2048, 512, 256
FLOPS = 2 * S * (K * H + H * N)

F32 = mybir.dt.float32
BF16 = mybir.dt.bfloat16
U32 = mybir.dt.uint32
U16 = mybir.dt.uint16
U8 = mybir.dt.uint8
FP8X4 = mybir.dt.float8_e4m3fn_x4
RELU = mybir.ActivationFunctionType.Relu
MULT = mybir.AluOpType.mult

P = 128
C = 512
NCH = S // C
ZCUTS = [0, 1023, 2048, 3071, 4096]


def tile_picked_place_mlp_relu_srt_l_kernel(tc, xT, w1, w2, gate, offs, out):
    nc = tc.nc
    x_hbm = xT.rearrange("(p j) s -> p j s", j=4)
    w1_hbm = w1.rearrange("(p j) c -> p j c", j=4)
    w2_hbm = w2.rearrange("(p j) c -> p j c", j=4)
    gate_hbm = gate.rearrange("(b p) s -> p b s", p=P)
    out_hbm = out.rearrange("(b p) t -> b p t", p=P)

    with ExitStack() as ctx:
        keep = ctx.enter_context(tc.tile_pool(name="keep", bufs=1))
        acc1 = ctx.enter_context(tc.psum_pool(name="acc1", bufs=6))
        acc2 = ctx.enter_context(tc.psum_pool(name="acc2", bufs=2))

        offsets = keep.tile([P, S // 16], U16, name="offsets")
        warm = keep.tile([P, 8], F32, name="warm")
        nc.gpsimd.memset(warm[:], 0.0)
        nc.scalar.activation(warm[:, 0:1], warm[:, 1:2], RELU)

        def load(name, shape, src):
            t = keep.tile(shape, F32, name=name, align_bytes=64)
            nc.sync.dma_start(out=t[:], in_=src)
            return t

        x_raw = {}
        g_raw = {}
        w1_raw = {}

        def load_x(c):
            x_raw[c] = load(f"x_raw{c}", [P, 4, C], x_hbm[:, :, C * c : C * c + C])

        def load_xh(c, h):
            if h == 0 or (c not in x_raw):
                x_raw[c] = x_raw.get(c) or keep.tile([P, 4, C], F32, name=f"x_raw{c}", align_bytes=64)
            a = 256 * h
            nc.sync.dma_start(out=x_raw[c][:, :, a : a + 256], in_=x_hbm[:, :, C * c + a : C * c + a + 256])

        def load_g(c):
            g_raw[c] = load(f"g_raw{c}", [P, 2, C], gate_hbm[:, :, C * c : C * c + C])

        def load_w1(i):
            w1_raw[i] = load(f"w1_raw{i}", [P, 4, 256], w1_hbm[:, :, 256 * i : 256 * i + 256])

        load_w1(1)
        load_w1(0)
        load_xh(0, 0)
        load_xh(0, 1)
        load_xh(1, 0)
        load_xh(1, 1)
        w2_raw = load("w2_raw", [P, 4, N], w2_hbm)
        load_x(2)
        load_x(3)
        nc.sync.dma_start(offsets[:], offs)
        load_g(0)
        load_g(1)
        load_g(2)
        load_g(3)

        windows = [keep.tile([P, T], F32, name=f"window{b}", align_bytes=64) for b in range(2)]
        w1_g = keep.tile([P, 4, P, 4], BF16, name="w1_g", align_bytes=64)
        w1_q = keep.tile([P, H], U32, name="w1_q", align_bytes=64)
        w1_s = keep.tile([P, H], U8, name="w1_s", align_bytes=64)
        w2_g = keep.tile([P, N, 4], BF16, name="w2_g", align_bytes=64)
        w2_q = keep.tile([P, N], U32, name="w2_q", align_bytes=64)
        w2_s = keep.tile([P, N], U8, name="w2_s", align_bytes=64)
        x_g = [keep.tile([P, C, 4], BF16, name=f"x_g{c}", align_bytes=64) for c in range(NCH)]
        x_q = [keep.tile([P, C], U32, name=f"x_q{c}", align_bytes=64) for c in range(NCH)]
        x_s = [keep.tile([P, C], U8, name=f"x_s{c}", align_bytes=64) for c in range(NCH)]
        h_g = [keep.tile([P, C, 4], BF16, name=f"h_g{c}", align_bytes=64) for c in range(NCH)]
        h_q = [keep.tile([P, C], U32, name=f"h_q{c}", align_bytes=64) for c in range(NCH)]
        h_s = [keep.tile([P, C], U8, name=f"h_s{c}", align_bytes=64) for c in range(NCH)]
        y = [[keep.tile([P, C], F32, name=f"y{c}_{b}", align_bytes=64) for b in range(2)] for c in range(NCH)]
        V, A = nc.vector.tensor_copy, nc.scalar.copy

        def ix(c, a, b, copy):
            copy(
                out=x_g[c][:, a:b, :],
                in_=x_raw[c][:, :, a:b].rearrange("p j n -> p n j"),
            )

        def qx(c, a=0, b=C):
            nc.vector.quantize_mx(
                out=x_q[c][:, a:b].bitcast(FP8X4), scales=x_s[c][:, a:b], in_=x_g[c][:, a:b, :].rearrange("p n j -> p (n j)")
            )

        def qh(c, a=0, b=C):
            nc.vector.quantize_mx(
                out=h_q[c][:, a:b].bitcast(FP8X4), scales=h_s[c][:, a:b], in_=h_g[c][:, a:b, :].rearrange("p n j -> p (n j)")
            )

        def iw1(i, copy):
            copy(
                out=w1_g[:, :, 64 * i : 64 * i + 64, :],
                in_=w1_raw[i][:].rearrange("p j (m t) -> p t m j", t=4),
            )

        def qw1():
            nc.vector.quantize_mx(out=w1_q[:].bitcast(FP8X4), scales=w1_s[:], in_=w1_g[:].rearrange("p t m j -> p (t m j)"))

        def w2p(copy=V):
            copy(
                out=w2_g[:], in_=w2_raw[:].rearrange("p j n -> p n j")
            )
            nc.vector.quantize_mx(out=w2_q[:].bitcast(FP8X4), scales=w2_s[:], in_=w2_g[:].rearrange("p n j -> p (n j)"))

        def z(i):
            engine = nc.gpsimd if i >= 4 else nc.vector
            a, b = ZCUTS[i % 4], ZCUTS[i % 4 + 1]
            engine.memset(windows[i // 4][:, a:b], 0.0)

        def l1(c, s, e):
            ps = acc1.tile([P, 4, P], F32, name="ps")
            for t in range(4):
                nc.tensor.matmul_mx(
                    out=ps[:, t, :],
                    lhsT=w1_q[:, P * t : P * t + P].bitcast(FP8X4),
                    lhsT_scale=w1_s[:, P * t : P * t + P],
                    rhs=x_q[c][:, P * s : P * s + P].bitcast(FP8X4),
                    rhs_scale=x_s[c][:, P * s : P * s + P],
                    start=True,
                    stop=True,
                )
            dst, src = h_g[c][:, P * s : P * s + P, :], ps[:].rearrange("p t n -> p n t")
            if e == 1:
                nc.vector.tensor_scalar_max(dst, src, 0.0)
            else:
                nc.scalar.activation(dst, src, RELU)

        def l2(c, b, copy):
            py = acc2.tile([P, C], F32, name="py")
            nc.tensor.matmul_mx(
                out=py[:],
                lhsT=w2_q[:, P * b : P * b + P].bitcast(FP8X4),
                lhsT_scale=w2_s[:, P * b : P * b + P],
                rhs=h_q[c][:].bitcast(FP8X4),
                rhs_scale=h_s[c][:],
                start=True,
                stop=True,
            )
            copy(out=y[c][b][:], in_=py[:])

        def sc(c, b, *stores):
            nc.vector.tensor_tensor(
                windows[b][:].indirect(offsets[:, C // 16 * c : C // 16 * (c + 1)]), y[c][b][:], g_raw[c][:, b, :], MULT
            )
            for lo, hi in stores:
                nc.sync.dma_start(out=out_hbm[b, :, lo:hi], in_=windows[b][:, lo:hi])

        ix(1, 0, 128, V)
        ix(1, 128, 256, A)
        qx(1, 0, 256)
        ix(0, 0, 128, V)
        ix(0, 128, 256, A)
        qx(0, 0, 256)
        ix(1, 256, 384, V)
        ix(1, 384, 512, A)
        qx(1, 256, 512)
        ix(0, 256, 384, V)
        ix(0, 384, 512, A)
        qx(0, 256, 512)
        z(0)
        z(1)
        z(2)
        z(3)
        z(4)
        z(5)
        z(6)
        z(7)
        iw1(0, V)
        iw1(1, A)
        qw1()
        ix(3, 0, 256, V)
        qx(3, 0, 256)
        l1(0, 2, 1)
        l1(0, 3, 0)
        w2p()
        l1(0, 0, 0)
        l1(0, 1, 0)
        l1(1, 0, 0)
        l1(1, 1, 0)
        qh(0)
        l2(0, 0, A)
        l1(1, 2, 0)
        l1(1, 3, 0)
        ix(2, 0, 256, V)
        qx(2, 0, 256)
        qh(1)
        l2(0, 1, A)
        ix(2, 256, 384, V)
        ix(2, 384, 512, A)
        qx(2, 256, 512)
        l2(1, 0, A)
        l1(2, 0, 0)
        l1(2, 1, 0)
        ix(3, 256, 512, V)
        qx(3, 256, 512)
        sc(0, 0)
        sc(1, 0, (0, 1024))
        l1(2, 2, 0)
        l1(2, 3, 0)
        l2(1, 1, A)
        sc(0, 1)
        qh(2)
        l1(3, 0, 0)
        l1(3, 1, 0)
        l1(3, 2, 0)
        l1(3, 3, 0)
        l2(2, 0, A)
        sc(1, 1, (0, 1024))
        qh(3)
        sc(2, 0)
        l2(2, 1, V)
        l2(3, 0, A)
        sc(3, 0, (1024, 4096))
        l2(3, 1, A)
        sc(2, 1)
        sc(3, 1, (1024, 4096))
